import numpy as np
import ml_dtypes


def mxq(x, axis, fmt="e4m3"):
    dtype, down = {"e4m3": (ml_dtypes.float8_e4m3fn, 7), "e5m2": (ml_dtypes.float8_e5m2, 14)}[fmt]
    v = np.moveaxis(np.asarray(x, np.float32).astype(ml_dtypes.bfloat16).astype(np.float64), axis, -1)
    blocks = v.reshape(v.shape[:-1] + (-1, 32))
    amax = np.abs(blocks).max(-1, keepdims=True)
    byte = np.maximum(np.where(amax > 0, np.frexp(amax)[1] - 1 + 127, 0) - down, 1)
    scale = np.exp2(byte - 127.0)
    codes = (blocks / scale).astype(np.float32).astype(dtype).astype(np.float64)
    return np.moveaxis((codes * scale).reshape(v.shape), -1, axis)


WIDE = False


def mx_kscale(k):
    if not WIDE:
        return np.ones(k)
    levels = np.array([10, -10, 5, -5, 0])
    if k % 512:
        return np.exp2(np.random.permutation(np.resize(levels, k // 32))).repeat(32)
    a = np.empty((k // 512, 16))
    for p in range(k // 512):
        a[p, :8] = np.random.permutation(np.resize(levels, 8))
        for g in range(8):
            far = levels[np.abs(levels - a[p, g]) >= 10]
            a[p, g + 8] = far[np.random.randint(len(far))]
    return np.exp2(a.ravel()).repeat(32)


def f64(x):
    return np.asarray(x).astype(np.float64)


def striped(idx):
    return np.tile(idx.reshape(-1, 16).T, (8, 1)).astype(np.uint16)


def unstriped(offs):
    return offs[:16].T.reshape(-1).astype(np.int64)


E2M1 = np.array([0.0, 0.5, 1.0, 1.5, 2.0, 3.0, 4.0, 6.0, -0.0, -0.5, -1.0, -1.5, -2.0, -3.0, -4.0, -6.0])


def pack_weight(w, fmt):
    k, n = w.shape
    w = f64(np.asarray(w, np.float32).astype(ml_dtypes.bfloat16)).reshape(k // 32, 32, n)
    amax = np.abs(w).max(1)
    if fmt == "e4m3":
        byte = np.frexp(amax)[1] - 1 + 127 - 7
    else:
        mant, ex = np.frexp(amax / 6.0)
        byte = np.where(mant > 0.5, ex, ex - 1) + 127
    byte = np.clip(np.where(amax > 0, byte, 1), 1, 254)
    scaled = (w * np.exp2(127.0 - byte)[:, None, :]).reshape(k, n).astype(np.float32)
    by_word = np.ascontiguousarray(scaled.reshape(k // 512, 128, 4, n).transpose(0, 1, 3, 2))
    if fmt == "e4m3":
        words = by_word.astype(ml_dtypes.float8_e4m3fn).view(np.uint8)
    else:
        c = by_word.astype(ml_dtypes.float4_e2m1fn).view(np.uint8) & 0xF
        words = (c[..., 0::2] | (c[..., 1::2] << 4)).reshape(k // 512, 128, 2 * n)
    return np.ascontiguousarray(words), np.ascontiguousarray(byte.astype(np.uint8).reshape(k // 512, 16, n))


def unpack_weight(words, scales, fmt):
    g, _, n = scales.shape
    words = np.ascontiguousarray(words).reshape(g, 128, n, -1)
    if fmt == "e4m3":
        vals = words.view(ml_dtypes.float8_e4m3fn).astype(np.float64)
    else:
        nib = np.empty((g, 128, n, 4), np.uint8)
        nib[..., 0::2] = words & 0xF
        nib[..., 1::2] = words >> 4
        vals = E2M1[nib]
    vals = vals * np.repeat(np.exp2(scales.astype(np.float64) - 127.0), 8, axis=1)[..., None]
    return vals.transpose(0, 1, 3, 2).reshape(g * 512, n)


def gelu(v):
    return 0.5 * v * (1.0 + np.tanh(np.sqrt(2.0 / np.pi) * (v + 0.044715 * v**3)))


K, H, T, S, T2, P = 1024, 1024, 2048, 512, 1024, 512

def setup_inputs():
    n = np.random.standard_normal
    s = mx_kscale(K)[:, None]
    u = mx_kscale(H)[:, None]
    d = {}
    d["tab_words"], d["tab_scales"] = pack_weight(n((K, T)) * s, "e4m3")
    d["offs"] = striped(np.random.permutation(T)[:S])
    d["offs2"] = striped(np.random.permutation(T2)[:S])
    d["offs3"] = striped(np.random.permutation(T2)[:P])
    d["w1"] = (n((K, H)) / K ** 0.5 / s * u.T).astype(np.float32)
    d["w2_words"], d["w2_scales"] = pack_weight(n((K, H)) / K ** 0.5 / s * u.T, "e2m1")
    d["w3_words"], d["w3_scales"] = pack_weight(n((K, H)) / K ** 0.5 / s * u.T, "e4m3")
    d["wgs"] = np.exp(0.3 * n((128, S))).astype(np.float32)
    d["page0"] = (n((H, T2)) * u).astype(np.float32)
    d["mat"] = (n((H, P)) * u).astype(np.float32)
    d["gv"] = (0.6 * np.sign(n(H)) * np.exp(0.3 * n(H)) / H ** 0.5 / u[:, 0] ** 2).astype(np.float32)
    d["slot"] = np.exp(0.5 * n(T2)).astype(np.float32)
    return d

def reference(tab_words, tab_scales, offs, offs2, offs3, w1, w2_words, w2_scales, w3_words, w3_scales, wgs, page0, mat, gv, slot):
    v = unpack_weight(tab_words, tab_scales, "e4m3")[:, unstriped(offs)]
    a = mxq(f64(w1), 0, "e4m3").T @ v
    b = unpack_weight(w2_words, w2_scales, "e2m1").T @ v
    d = unpack_weight(w3_words, w3_scales, "e4m3").T @ v
    h = np.minimum(a, b) + d
    page = f64(page0).copy()
    page[:, unstriped(offs2)] = np.tile(f64(wgs), (H // 128, 1)) * h
    x = (page[:, unstriped(offs3)] + f64(mat)) * f64(gv)[:, None]
    e = mxq(page, 0, "e4m3").T @ mxq(x, 0, "e4m3")
    return np.log(np.square(e) + f64(slot)[:, None])

@@ -1,0 +1,320 @@
+from contextlib import ExitStack
+
+import concourse.mybir as mybir
+
+K, H, T, S, T2, NX = 1024, 1024, 2048, 512, 1024, 512
+FLOPS = 2 * (3 * K * H * S + H * T2 * NX)
+
+F32 = mybir.dt.float32
+BF16 = mybir.dt.bfloat16
+I32 = mybir.dt.int32
+U32 = mybir.dt.uint32
+U16 = mybir.dt.uint16
+U8 = mybir.dt.uint8
+FP8X4 = mybir.dt.float8_e4m3fn_x4
+FP4X4 = mybir.dt.float4_e2m1fn_x4
+ALU = mybir.AluOpType
+ACT = mybir.ActivationFunctionType
+
+P = 128
+PACK = 4
+KP = P * PACK
+PASSES = K // KP
+HALVES = H // KP
+SLICES = HALVES * PACK
+CHUNK = 256
+SQUARES_ON_SCALAR = (0, 1, 2, 3)
+
+
+def tile_list_lottery_terminal_desk_kernel(
+    tc, tab_words, tab_scales, offs, offs2, offs3, w1, w2_words, w2_scales, w3_words, w3_scales, wgs, page0, mat, gv, slot, out
+):
+    nc = tc.nc
+    with ExitStack() as ctx:
+        keep = ctx.enter_context(tc.tile_pool(name="keep", bufs=1))
+        ring2 = ctx.enter_context(tc.tile_pool(name="ring2", bufs=2))
+        ring4 = ctx.enter_context(tc.tile_pool(name="ring4", bufs=4))
+        psum = ctx.enter_context(tc.psum_pool(name="psum", bufs=1))
+
+        list1 = keep.tile([P, S // 16], U16, name="list1")
+        list2 = keep.tile([P, S // 16], U16, name="list2")
+        list3 = keep.tile([P, NX // 16], U16, name="list3")
+        tab_w = [keep.tile([P, T], I32, name="tab_w%d" % a, align_bytes=64) for a in range(PASSES)]
+        tab_s = keep.tile([P, PASSES * T], U8, name="tab_s", align_bytes=64)
+        ws_raw = keep.tile([P, PASSES, H], U8, name="ws_raw", align_bytes=64)
+        nc.gpsimd.memset(tab_s[:].bitcast(I32), 0)
+        nc.vector.memset(ws_raw[:].bitcast(I32), 0)
+        warm = keep.tile([P, 2], F32, name="warm")
+        nc.gpsimd.memset(warm[:], 1.0)
+        nc.scalar.activation(warm[:, 1:2], warm[:, 0:1], ACT.Ln)
+
+        w2_raw = [keep.tile([P, PASSES, KP // 2], I32, name="w2_raw%d" % b, align_bytes=64) for b in range(HALVES)]
+        w3_raw = [keep.tile([P, PASSES, KP], I32, name="w3_raw%d" % b, align_bytes=64) for b in range(HALVES)]
+        wg = [keep.tile([P, S], F32, name="wg%d" % t) for t in range(PACK)]
+        page = [keep.tile([P, T2], F32, name="page%d" % s) for s in range(SLICES)]
+        mats = [keep.tile([P, NX], F32, name="mat%d" % s) for s in range(SLICES)]
+        gv_sb = keep.tile([P, HALVES, PACK], F32, name="gv_sb")
+        slot_sb = keep.tile([P, T2 // P], F32, name="slot_sb")
+        w1_raw = {}
+
+        def load_tab(a):
+            nc.sync.dma_start(tab_w[a][:], tab_words[a].rearrange("p n i -> p (n i)").bitcast(I32))
+
+        def load_tab_scales():
+            for q in range(4):
+                nc.sync.dma_start(
+                    tab_s[32 * q : 32 * q + 4, :].bitcast(I32).rearrange("p (a n) -> p a n", a=PASSES),
+                    tab_scales[:, 4 * q : 4 * q + 4, :].rearrange("a r n -> r a n").bitcast(I32),
+                )
+
+        def load_weight_scales(scales, row0):
+            for q in range(4):
+                nc.sync.dma_start(
+                    ws_raw[32 * q + row0 : 32 * q + row0 + 4, :, :].bitcast(I32),
+                    scales[:, 4 * q : 4 * q + 4, :].rearrange("a r n -> r a n").bitcast(I32),
+                )
+
+        def load_w1(a, b):
+            raw = ring2.tile([P, PACK, KP], F32, name="w1_raw")
+            nc.sync.dma_start(raw[:], w1[KP * a : KP * (a + 1), KP * b : KP * (b + 1)].rearrange("(p j) c -> p j c", j=PACK))
+            w1_raw[a, b] = raw
+
+        def load_w3(b):
+            nc.sync.dma_start(
+                w3_raw[b][:], w3_words.rearrange("a p c i -> p a (c i)")[:, :, 4 * KP * b : 4 * KP * (b + 1)].bitcast(I32)
+            )
+
+        def load_w2(b):
+            nc.sync.dma_start(
+                w2_raw[b][:], w2_words.rearrange("a p c -> p a c")[:, :, 2 * KP * b : 2 * KP * (b + 1)].bitcast(I32)
+            )
+
+        def load_wg(t):
+            rows = wgs.rearrange("(p t) j -> t p j", t=PACK)[t]
+            for q in range(4):
+                nc.sync.dma_start(wg[t][32 * q : 32 * (q + 1), :], rows)
+
+        def load_slice(s):
+            b, t = divmod(s, PACK)
+            nc.sync.dma_start(page[s][:], page0.rearrange("(b p t) m -> b t p m", b=HALVES, t=PACK)[b, t])
+            nc.sync.dma_start(mats[s][:], mat.rearrange("(b p t) j -> b t p j", b=HALVES, t=PACK)[b, t])
+
+        nc.sync.dma_start(list1[:], offs)
+        load_tab(0)
+        load_tab_scales()
+        load_w1(0, 0)
+        load_weight_scales(w2_scales, 0)
+        load_w2(0)
+        load_tab(1)
+        load_weight_scales(w3_scales, 4)
+        load_w1(1, 0)
+        load_w3(0)
+        nc.sync.dma_start(list2[:], offs2)
+        load_wg(0)
+        nc.sync.dma_start(list3[:], offs3)
+        load_slice(0)
+        with nc.allow_non_contiguous_dma(reason="one value of gv for each row of a slice"):
+            nc.sync.dma_start(gv_sb[:], gv.rearrange("(b p t) -> p b t", b=HALVES, t=PACK))
+        load_wg(1)
+        load_slice(1)
+
+        v_codes, v_scales = [], []
+        for a in range(PASSES):
+            codes = keep.tile([P, S], U32, name="v_codes%d" % a, align_bytes=64)
+            scales = keep.tile([P, S], U8, name="v_scales%d" % a, align_bytes=64)
+            nc.vector.tensor_copy(codes[:], tab_w[a][:].bitcast(U32).indirect(list1[:]))
+            nc.vector.tensor_copy(scales[:], tab_s[:, T * a : T * (a + 1)].indirect(list1[:]))
+            v_codes.append(codes)
+            v_scales.append(scales)
+
+        def deal(dst, src, run):
+            nc.vector.tensor_copy(
+                dst.rearrange("p a (t c i) -> p a c t i", t=PACK, i=run),
+                src.rearrange("p a (c i t) -> p a c t i", t=PACK, i=run),
+            )
+
+        w1_codes, w1_scales, w2_codes, w3_codes, w_scales = {}, {}, {}, {}, {}
+
+        def deal_w3(b):
+            w3_codes[b] = keep.tile([P, PASSES, KP], I32, name="w3_codes%d" % b, align_bytes=64)
+            deal(w3_codes[b][:], w3_raw[b][:], 4)
+
+        def deal_w2(b):
+            w2_codes[b] = keep.tile([P, PASSES, KP // 2], I32, name="w2_codes%d" % b, align_bytes=64)
+            deal(w2_codes[b][:].bitcast(U16), w2_raw[b][:].bitcast(U16), 8)
+            w_scales[b] = keep.tile([P, PASSES, KP], U8, name="w_scales%d" % b, align_bytes=64)
+            deal(w_scales[b][:], ws_raw[:, :, KP * b : KP * (b + 1)], 16)
+
+        def round_w1(a, b, vector_from):
+            grouped = ring2.tile([P, KP * PACK], BF16, name="grouped", align_bytes=64)
+            dst = grouped[:].rearrange("p (t m j) -> p m t j", t=PACK, j=PACK)
+            src = w1_raw[a, b][:].rearrange("p j (m t) -> p m t j", t=PACK)
+            nc.scalar.copy(dst[:, :vector_from], src[:, :vector_from])
+            if vector_from < P:
+                nc.vector.tensor_copy(dst[:, vector_from:], src[:, vector_from:])
+            return grouped
+
+        def quantize_w1(a, b, grouped):
+            w1_codes[a, b] = keep.tile([P, KP], U32, name="w1_codes%d%d" % (a, b), align_bytes=64)
+            w1_scales[a, b] = keep.tile([P, KP], U8, name="w1_scales%d%d" % (a, b), align_bytes=64)
+            nc.vector.quantize_mx(out=w1_codes[a, b][:].bitcast(FP8X4), scales=w1_scales[a, b][:], in_=grouped[:])
+
+        def bank(n):
+            return psum.tile([P, 512], F32, name="bank%d" % (n % 8))
+
+        h = {}
+
+        sums = {}
+
+        def first_stage(s):
+            products(s)
+            combine(s)
+
+        def products(s):
+            b, t = divmod(s, PACK)
+            cols = slice(P * t, P * (t + 1))
+            sum2, sum3, sum1 = bank(3 * s), bank(3 * s + 1), bank(3 * s + 2)
+            for acc, codes, scales in (
+                (sum2, lambda a: w2_codes[b][:, a, P // 2 * t : P // 2 * (t + 1)].bitcast(FP4X4), lambda a: w_scales[b][:, a, cols]),
+                (sum1, lambda a: w1_codes[a, b][:, cols].bitcast(FP8X4), lambda a: w1_scales[a, b][:, cols]),
+                (sum3, lambda a: w3_codes[b][:, a, cols].bitcast(FP8X4), lambda a: w_scales[b][4:P, a, cols]),
+            ):
+                for a in range(PASSES):
+                    nc.tensor.matmul_mx(
+                        out=acc[:], lhsT=codes(a), lhsT_scale=scales(a),
+                        rhs=v_codes[a][:].bitcast(FP8X4), rhs_scale=v_scales[a][:],
+                        start=(a == 0), stop=(a == PASSES - 1),
+                    )
+            second = ring2.tile([P, S], F32, name="second")
+            nc.scalar.copy(second[:], sum2[:])
+            sums[s] = (sum1, second, sum3)
+
+        def combine(s):
+            sum1, second, sum3 = sums[s]
+            if s == SLICES - 1:
+                least = keep.tile([P, S], F32, name="page_grouped%d" % (T2 // CHUNK - 1), align_bytes=64)
+                h[s] = keep.tile([P, S], F32, name="mat%d" % (s - 1))
+            else:
+                least = ring2.tile([P, S], F32, name="least")
+                h[s] = ring4.tile([P, S], F32, name="h")
+            nc.vector.tensor_tensor(least[:], sum1[:], second[:], ALU.min)
+            nc.vector.tensor_tensor(h[s][:], sum3[:], least[:], ALU.add)
+
+        page_bf, x_bf = {}, {}
+
+        def put_and_fetch(s):
+            b, t = divmod(s, PACK)
+            if t == 0:
+                page_bf[b] = ring2.tile([P, PACK, T2], BF16, name="page_bf", align_bytes=64)
+                x_bf[b] = ring2.tile([P, PACK, NX], BF16, name="x_bf", align_bytes=64)
+            nc.vector.tensor_tensor(page[s][:].indirect(list2[:]), h[s][:], wg[t][:], ALU.mult)
+            shifted = ring4.tile([P, NX], F32, name="shifted")
+            nc.vector.tensor_tensor(shifted[:], page[s][:].indirect(list3[:]), mats[s][:], ALU.add)
+            nc.scalar.copy(page_bf[b][:, t, :], page[s][:])
+            if s == SLICES - 1:
+                nc.vector.tensor_scalar(x_bf[b][:, t, :], shifted[:], gv_sb[:, b, t : t + 1], None, ALU.mult)
+            else:
+                nc.scalar.activation(x_bf[b][:, t, :], shifted[:], ACT.Copy, scale=gv_sb[:, b, t : t + 1])
+
+        def interleave(copy, dst, src):
+            copy(dst.rearrange("p (c i t) -> p c t i", t=PACK, i=4), src.rearrange("p t (c i) -> p c t i", i=4))
+
+        page_codes, page_scales, x_codes, x_scales = {}, {}, {}, {}
+
+        x_grouped, page_grouped = {}, {}
+
+        def group_half(b):
+            last = b == HALVES - 1
+            x_grouped[b] = ring2.tile([P, NX * PACK], BF16, name="grouped", align_bytes=64)
+            interleave(nc.vector.tensor_copy if last else nc.scalar.copy, x_grouped[b][:], x_bf[b][:])
+            for c in range(T2 // CHUNK):
+                grouped = keep.tile([P, CHUNK * PACK], BF16, name="page_grouped%d" % c, align_bytes=64)
+                on_vector = last and c == T2 // CHUNK - 1
+                interleave(
+                    nc.vector.tensor_copy if on_vector else nc.scalar.copy, grouped[:], page_bf[b][:, :, CHUNK * c : CHUNK * (c + 1)]
+                )
+                page_grouped[b, c] = grouped
+
+        def quantize_half(b):
+            x_codes[b] = keep.tile([P, NX], U32, name="x_codes%d" % b, align_bytes=64)
+            x_scales[b] = keep.tile([P, NX], U8, name="x_scales%d" % b, align_bytes=64)
+            nc.vector.quantize_mx(out=x_codes[b][:].bitcast(FP8X4), scales=x_scales[b][:], in_=x_grouped[b][:])
+            for c in range(T2 // CHUNK):
+                grouped = page_grouped[b, c]
+                page_codes[b, c] = keep.tile([P, CHUNK], U32, name="page_codes%d%d" % (b, c), align_bytes=64)
+                page_scales[b, c] = keep.tile([P, CHUNK], U8, name="page_scales%d%d" % (b, c), align_bytes=64)
+                nc.vector.quantize_mx(out=page_codes[b, c][:].bitcast(FP8X4), scales=page_scales[b, c][:], in_=grouped[:])
+
+        scores = {}
+
+        def second_stage(b):
+            for n in range(T2 // P):
+                c, off = divmod(P * n, CHUNK)
+                if b == 0:
+                    scores[n] = bank(n)
+                nc.tensor.matmul_mx(
+                    out=scores[n][:],
+                    lhsT=page_codes[b, c][:, off : off + P].bitcast(FP8X4), lhsT_scale=page_scales[b, c][:, off : off + P],
+                    rhs=x_codes[b][:].bitcast(FP8X4), rhs_scale=x_scales[b][:],
+                    start=(b == 0), stop=(b == HALVES - 1),
+                )
+
+        grouped0 = round_w1(0, 0, P)
+        deal_w2(0)
+        quantize_w1(0, 0, grouped0)
+        quantize_w1(1, 0, round_w1(1, 0, 44))
+        deal_w3(0)
+
+        load_w1(0, 1)
+        load_w1(1, 1)
+        load_w3(1)
+        load_w2(1)
+        load_wg(2)
+        load_slice(2)
+        load_wg(3)
+        for s in range(3, SLICES):
+            load_slice(s)
+        with nc.allow_non_contiguous_dma(reason="one value of slot for each output row"):
+            nc.sync.dma_start(slot_sb[:], slot.rearrange("(n p) -> p n", p=P))
+
+        first_stage(0)
+        first_stage(1)
+        put_and_fetch(0)
+        first_stage(2)
+        first_stage(3)
+        put_and_fetch(1)
+        grouped0 = round_w1(0, 1, P)
+        grouped1 = round_w1(1, 1, P)
+        deal_w2(1)
+        deal_w3(1)
+        quantize_w1(0, 1, grouped0)
+        quantize_w1(1, 1, grouped1)
+        put_and_fetch(2)
+        first_stage(4)
+        first_stage(5)
+        put_and_fetch(3)
+        first_stage(6)
+        products(7)
+        group_half(0)
+        put_and_fetch(4)
+        put_and_fetch(5)
+        put_and_fetch(6)
+        quantize_half(0)
+        combine(7)
+        second_stage(0)
+        put_and_fetch(7)
+        group_half(1)
+        quantize_half(1)
+        second_stage(1)
+
+        for n in range(T2 // P):
+            square = ring2.tile([P, NX], F32, name="square")
+            if n in SQUARES_ON_SCALAR:
+                nc.scalar.activation(square[:], scores[n][:], ACT.Square)
+            else:
+                plain = ring2.tile([P, NX], F32, name="second")
+                nc.vector.tensor_copy(plain[:], scores[n][:])
+                nc.vector.tensor_tensor(square[:], scores[n][:], plain[:], ALU.mult)
+            result = ring4.tile([P, NX], F32, name="result")
+            nc.scalar.activation(result[:], square[:], ACT.Ln, bias=slot_sb[:, n : n + 1])
+            nc.sync.dma_start(out[P * n : P * (n + 1), :], result[:])

@@ -1,6 +1,7 @@
 from contextlib import ExitStack
 
 import concourse.mybir as mybir
+from concourse.masks import make_identity
 
 K, H, T, S, T2, NX = 1024, 1024, 2048, 512, 1024, 512
 FLOPS = 2 * (3 * K * H * S + H * T2 * NX)
@@ -22,8 +23,13 @@ KP = P * PACK
 PASSES = K // KP
 HALVES = H // KP
 SLICES = HALVES * PACK
+ENTRY_TILES = S // P
 CHUNK = 256
-SQUARES_ON_SCALAR = (0, 1, 2, 3)
+CHUNKS = T2 // CHUNK
+W1_COLS = 256
+W1_PIECES = KP // W1_COLS
+W3_ROW = 8
+SQUARES_ON_SCALAR = (0, 1, 3, 5)
 
 
 def tile_list_lottery_terminal_desk_kernel(
@@ -41,16 +47,20 @@ def tile_list_lottery_terminal_desk_kernel(
         list3 = keep.tile([P, NX // 16], U16, name="list3")
         tab_w = [keep.tile([P, T], I32, name="tab_w%d" % a, align_bytes=64) for a in range(PASSES)]
         tab_s = keep.tile([P, PASSES * T], U8, name="tab_s", align_bytes=64)
-        ws_raw = keep.tile([P, PASSES, H], U8, name="ws_raw", align_bytes=64)
+        w2_planes = [keep.tile([P, PASSES, KP], U8, name="w2_planes%d" % b, align_bytes=64) for b in range(HALVES)]
+        w3_planes = [keep.tile([P, KP], U8, name="w3_planes%d" % b, align_bytes=64) for b in range(HALVES)]
         nc.gpsimd.memset(tab_s[:].bitcast(I32), 0)
-        nc.vector.memset(ws_raw[:].bitcast(I32), 0)
+        for planes in (w2_planes[0], w3_planes[0], w2_planes[1], w3_planes[1]):
+            nc.vector.memset(planes[:].bitcast(I32), 0)
         warm = keep.tile([P, 2], F32, name="warm")
-        nc.gpsimd.memset(warm[:], 1.0)
+        nc.vector.memset(warm[:], 1.0)
         nc.scalar.activation(warm[:, 1:2], warm[:, 0:1], ACT.Ln)
 
-        w2_raw = [keep.tile([P, PASSES, KP // 2], I32, name="w2_raw%d" % b, align_bytes=64) for b in range(HALVES)]
-        w3_raw = [keep.tile([P, PASSES, KP], I32, name="w3_raw%d" % b, align_bytes=64) for b in range(HALVES)]
-        wg = [keep.tile([P, S], F32, name="wg%d" % t) for t in range(PACK)]
+        w2_codes = [keep.tile([P, PASSES, KP // 2], I32, name="w2_codes%d" % b, align_bytes=64) for b in range(HALVES)]
+        w3_codes = [keep.tile([P, PASSES, KP], I32, name="w3_codes%d" % b, align_bytes=64) for b in range(HALVES)]
+        wg_first = keep.tile([P, S], F32, name="wg_first")
+        wg_rest = keep.tile([P, (PACK - 1) * S], F32, name="wg_rest")
+        wg = [wg_first[:]] + [wg_rest[:, S * t : S * (t + 1)] for t in range(PACK - 1)]
         page = [keep.tile([P, T2], F32, name="page%d" % s) for s in range(SLICES)]
         mats = [keep.tile([P, NX], F32, name="mat%d" % s) for s in range(SLICES)]
         gv_sb = keep.tile([P, HALVES, PACK], F32, name="gv_sb")
@@ -61,189 +71,214 @@ def tile_list_lottery_terminal_desk_kernel(
             nc.sync.dma_start(tab_w[a][:], tab_words[a].rearrange("p n i -> p (n i)").bitcast(I32))
 
         def load_tab_scales():
-            for q in range(4):
+            for r in range(4):
                 nc.sync.dma_start(
-                    tab_s[32 * q : 32 * q + 4, :].bitcast(I32).rearrange("p (a n) -> p a n", a=PASSES),
-                    tab_scales[:, 4 * q : 4 * q + 4, :].rearrange("a r n -> r a n").bitcast(I32),
+                    tab_s[r:P:32, :].bitcast(I32).rearrange("q (a n) -> q a n", a=PASSES),
+                    tab_scales.rearrange("a (q r) n -> r q a n", r=4)[r].bitcast(I32),
                 )
 
-        def load_weight_scales(scales, row0):
-            for q in range(4):
+        def load_w2_planes(b):
+            for r in range(4):
                 nc.sync.dma_start(
-                    ws_raw[32 * q + row0 : 32 * q + row0 + 4, :, :].bitcast(I32),
-                    scales[:, 4 * q : 4 * q + 4, :].rearrange("a r n -> r a n").bitcast(I32),
+                    w2_planes[b][r:P:32, :, :].bitcast(I32),
+                    w2_scales.rearrange("a (q r) n -> r q a n", r=4)[r][:, :, KP * b : KP * (b + 1)].bitcast(I32),
                 )
 
-        def load_w1(a, b):
-            raw = ring2.tile([P, PACK, KP], F32, name="w1_raw")
-            nc.sync.dma_start(raw[:], w1[KP * a : KP * (a + 1), KP * b : KP * (b + 1)].rearrange("(p j) c -> p j c", j=PACK))
-            w1_raw[a, b] = raw
+        def load_w3_planes(b):
+            for q in range(4):
+                nc.sync.dma_start(
+                    w3_planes[b][32 * q + W3_ROW : 32 * q + W3_ROW + 8, :].bitcast(I32),
+                    w3_scales[:, 4 * q : 4 * q + 4, KP * b : KP * (b + 1)].bitcast(I32),
+                )
+
+        def load_wg(tile, cols):
+            rows = wgs.rearrange("(p t) j -> p (t j)", t=PACK)[:, cols]
+            for q in range(4):
+                nc.sync.dma_start(tile[32 * q : 32 * (q + 1), :], rows)
+
+        def load_w1(a, b, u):
+            w1_raw[a, b, u] = keep.tile([P, PACK, W1_COLS], F32, name="w1_raw%d%d%d" % (a, b, u))
+            c0 = KP * b + W1_COLS * u
+            rows = w1[KP * a : KP * (a + 1), c0 : c0 + W1_COLS]
+            nc.sync.dma_start(w1_raw[a, b, u][:], rows.rearrange("(p j) c -> p j c", j=PACK))
 
         def load_w3(b):
             nc.sync.dma_start(
-                w3_raw[b][:], w3_words.rearrange("a p c i -> p a (c i)")[:, :, 4 * KP * b : 4 * KP * (b + 1)].bitcast(I32)
+                w3_codes[b][:], w3_words.rearrange("a p c i -> p a (c i)")[:, :, 4 * KP * b : 4 * KP * (b + 1)].bitcast(I32)
             )
 
         def load_w2(b):
             nc.sync.dma_start(
-                w2_raw[b][:], w2_words.rearrange("a p c -> p a c")[:, :, 2 * KP * b : 2 * KP * (b + 1)].bitcast(I32)
+                w2_codes[b][:], w2_words.rearrange("a p c -> p a c")[:, :, 2 * KP * b : 2 * KP * (b + 1)].bitcast(I32)
             )
 
-        def load_wg(t):
-            rows = wgs.rearrange("(p t) j -> t p j", t=PACK)[t]
-            for q in range(4):
-                nc.sync.dma_start(wg[t][32 * q : 32 * (q + 1), :], rows)
-
-        def load_slice(s):
+        def load_page(s):
             b, t = divmod(s, PACK)
             nc.sync.dma_start(page[s][:], page0.rearrange("(b p t) m -> b t p m", b=HALVES, t=PACK)[b, t])
+
+        def load_mat(s):
+            b, t = divmod(s, PACK)
             nc.sync.dma_start(mats[s][:], mat.rearrange("(b p t) j -> b t p j", b=HALVES, t=PACK)[b, t])
 
         nc.sync.dma_start(list1[:], offs)
         load_tab(0)
         load_tab_scales()
-        load_w1(0, 0)
-        load_weight_scales(w2_scales, 0)
-        load_w2(0)
         load_tab(1)
-        load_weight_scales(w3_scales, 4)
-        load_w1(1, 0)
+        load_w2(0)
+        load_w2_planes(0)
         load_w3(0)
+        load_w1(0, 0, 0)
+        load_w3_planes(0)
+        load_w1(0, 0, 1)
+        load_w1(1, 0, 0)
+        load_w1(1, 0, 1)
+        identity = keep.tile([P, P], F32, name="identity")
+        make_identity(nc, identity[:])
         nc.sync.dma_start(list2[:], offs2)
-        load_wg(0)
+        nc.sync.dma_start(gv_sb[:], gv.rearrange("(b p t) -> p b t", b=HALVES, t=PACK))
+        load_page(0)
+        load_wg(wg_first, slice(0, S))
         nc.sync.dma_start(list3[:], offs3)
-        load_slice(0)
-        with nc.allow_non_contiguous_dma(reason="one value of gv for each row of a slice"):
-            nc.sync.dma_start(gv_sb[:], gv.rearrange("(b p t) -> p b t", b=HALVES, t=PACK))
-        load_wg(1)
-        load_slice(1)
+        load_mat(0)
 
-        v_codes, v_scales = [], []
+        v_codes = [keep.tile([P, S], U32, name="v_codes%d" % a, align_bytes=64) for a in range(PASSES)]
+        v_scales = [keep.tile([P, S], U8, name="v_scales%d" % a, align_bytes=64) for a in range(PASSES)]
         for a in range(PASSES):
-            codes = keep.tile([P, S], U32, name="v_codes%d" % a, align_bytes=64)
-            scales = keep.tile([P, S], U8, name="v_scales%d" % a, align_bytes=64)
-            nc.vector.tensor_copy(codes[:], tab_w[a][:].bitcast(U32).indirect(list1[:]))
-            nc.vector.tensor_copy(scales[:], tab_s[:, T * a : T * (a + 1)].indirect(list1[:]))
-            v_codes.append(codes)
-            v_scales.append(scales)
-
-        def deal(dst, src, run):
-            nc.vector.tensor_copy(
-                dst.rearrange("p a (t c i) -> p a c t i", t=PACK, i=run),
-                src.rearrange("p a (c i t) -> p a c t i", t=PACK, i=run),
-            )
-
-        w1_codes, w1_scales, w2_codes, w3_codes, w_scales = {}, {}, {}, {}, {}
-
-        def deal_w3(b):
-            w3_codes[b] = keep.tile([P, PASSES, KP], I32, name="w3_codes%d" % b, align_bytes=64)
-            deal(w3_codes[b][:], w3_raw[b][:], 4)
-
-        def deal_w2(b):
-            w2_codes[b] = keep.tile([P, PASSES, KP // 2], I32, name="w2_codes%d" % b, align_bytes=64)
-            deal(w2_codes[b][:].bitcast(U16), w2_raw[b][:].bitcast(U16), 8)
-            w_scales[b] = keep.tile([P, PASSES, KP], U8, name="w_scales%d" % b, align_bytes=64)
-            deal(w_scales[b][:], ws_raw[:, :, KP * b : KP * (b + 1)], 16)
-
-        def round_w1(a, b, vector_from):
-            grouped = ring2.tile([P, KP * PACK], BF16, name="grouped", align_bytes=64)
-            dst = grouped[:].rearrange("p (t m j) -> p m t j", t=PACK, j=PACK)
-            src = w1_raw[a, b][:].rearrange("p j (m t) -> p m t j", t=PACK)
-            nc.scalar.copy(dst[:, :vector_from], src[:, :vector_from])
-            if vector_from < P:
-                nc.vector.tensor_copy(dst[:, vector_from:], src[:, vector_from:])
-            return grouped
-
-        def quantize_w1(a, b, grouped):
-            w1_codes[a, b] = keep.tile([P, KP], U32, name="w1_codes%d%d" % (a, b), align_bytes=64)
-            w1_scales[a, b] = keep.tile([P, KP], U8, name="w1_scales%d%d" % (a, b), align_bytes=64)
-            nc.vector.quantize_mx(out=w1_codes[a, b][:].bitcast(FP8X4), scales=w1_scales[a, b][:], in_=grouped[:])
-
-        def bank(n):
-            return psum.tile([P, 512], F32, name="bank%d" % (n % 8))
-
-        h = {}
-
-        sums = {}
-
-        def first_stage(s):
-            products(s)
-            combine(s)
-
-        def products(s):
-            b, t = divmod(s, PACK)
-            cols = slice(P * t, P * (t + 1))
-            sum2, sum3, sum1 = bank(3 * s), bank(3 * s + 1), bank(3 * s + 2)
-            for acc, codes, scales in (
-                (sum2, lambda a: w2_codes[b][:, a, P // 2 * t : P // 2 * (t + 1)].bitcast(FP4X4), lambda a: w_scales[b][:, a, cols]),
-                (sum1, lambda a: w1_codes[a, b][:, cols].bitcast(FP8X4), lambda a: w1_scales[a, b][:, cols]),
-                (sum3, lambda a: w3_codes[b][:, a, cols].bitcast(FP8X4), lambda a: w_scales[b][4:P, a, cols]),
-            ):
-                for a in range(PASSES):
-                    nc.tensor.matmul_mx(
-                        out=acc[:], lhsT=codes(a), lhsT_scale=scales(a),
-                        rhs=v_codes[a][:].bitcast(FP8X4), rhs_scale=v_scales[a][:],
-                        start=(a == 0), stop=(a == PASSES - 1),
-                    )
-            second = ring2.tile([P, S], F32, name="second")
-            nc.scalar.copy(second[:], sum2[:])
-            sums[s] = (sum1, second, sum3)
-
-        def combine(s):
-            sum1, second, sum3 = sums[s]
-            if s == SLICES - 1:
-                least = keep.tile([P, S], F32, name="page_grouped%d" % (T2 // CHUNK - 1), align_bytes=64)
-                h[s] = keep.tile([P, S], F32, name="mat%d" % (s - 1))
-            else:
-                least = ring2.tile([P, S], F32, name="least")
-                h[s] = ring4.tile([P, S], F32, name="h")
-            nc.vector.tensor_tensor(least[:], sum1[:], second[:], ALU.min)
-            nc.vector.tensor_tensor(h[s][:], sum3[:], least[:], ALU.add)
-
-        page_bf, x_bf = {}, {}
-
-        def put_and_fetch(s):
-            b, t = divmod(s, PACK)
-            if t == 0:
-                page_bf[b] = ring2.tile([P, PACK, T2], BF16, name="page_bf", align_bytes=64)
-                x_bf[b] = ring2.tile([P, PACK, NX], BF16, name="x_bf", align_bytes=64)
-            nc.vector.tensor_tensor(page[s][:].indirect(list2[:]), h[s][:], wg[t][:], ALU.mult)
-            shifted = ring4.tile([P, NX], F32, name="shifted")
-            nc.vector.tensor_tensor(shifted[:], page[s][:].indirect(list3[:]), mats[s][:], ALU.add)
-            nc.scalar.copy(page_bf[b][:, t, :], page[s][:])
-            if s == SLICES - 1:
-                nc.vector.tensor_scalar(x_bf[b][:, t, :], shifted[:], gv_sb[:, b, t : t + 1], None, ALU.mult)
-            else:
-                nc.scalar.activation(x_bf[b][:, t, :], shifted[:], ACT.Copy, scale=gv_sb[:, b, t : t + 1])
+            nc.vector.tensor_copy(v_codes[a][:], tab_w[a][:].bitcast(U32).indirect(list1[:]))
+            nc.vector.tensor_copy(v_scales[a][:], tab_s[:, T * a : T * (a + 1)].indirect(list1[:]))
 
         def interleave(copy, dst, src):
             copy(dst.rearrange("p (c i t) -> p c t i", t=PACK, i=4), src.rearrange("p t (c i) -> p c t i", i=4))
 
-        page_codes, page_scales, x_codes, x_scales = {}, {}, {}, {}
+        w1_codes, w1_scales, w1_grouped = {}, {}, {}
 
+        def round_w1(a, b, u, copy, grouped):
+            interleave(copy, grouped[:], w1_raw[a, b, u][:])
+            w1_grouped[a, b, u] = grouped
+
+        def quantize_w1(a, b):
+            w1_codes[a, b] = keep.tile([P, KP], U32, name="h%d" % (a + 1) if b else "w1_codes%d" % a, align_bytes=64)
+            w1_scales[a, b] = keep.tile([P, KP], U8, name="w1_scales%d%d" % (a, b), align_bytes=64)
+            for u in range(W1_PIECES):
+                cols = slice(W1_COLS * u, W1_COLS * (u + 1))
+                nc.vector.quantize_mx(
+                    out=w1_codes[a, b][:, cols].bitcast(FP8X4), scales=w1_scales[a, b][:, cols], in_=w1_grouped[a, b, u][:]
+                )
+
+        def bank(n):
+            return psum.tile([P, 512], F32, name="bank%d" % n)
+
+        def by_row(tile):
+            return tile[:].rearrange("p (m t) -> p m t", t=PACK)
+
+        def dealt(tile):
+            return tile[:].rearrange("p t m -> p m t")
+
+        def one_pass(acc, e, a, codes, scales):
+            entries = slice(P * e, P * (e + 1))
+            nc.tensor.matmul_mx(
+                out=acc[:], lhsT=v_codes[a][:, entries].bitcast(FP8X4), lhsT_scale=v_scales[a][:, entries],
+                rhs=codes, rhs_scale=scales, start=(a == 0), stop=(a == PASSES - 1),
+            )
+
+        first, second, third, least, turned, h = {}, {}, {}, {}, {}, {}
+
+        def given_products(b):
+            sums2 = [bank(e) for e in range(ENTRY_TILES)]
+            sums3 = [bank(ENTRY_TILES + e) for e in range(ENTRY_TILES)]
+            for a in range(PASSES):
+                for e in range(ENTRY_TILES):
+                    one_pass(sums2[e], e, a, w2_codes[b][:, a, :].bitcast(FP4X4), w2_planes[b][:, a, :])
+                for e in range(ENTRY_TILES):
+                    one_pass(sums3[e], e, a, w3_codes[b][:, a, :].bitcast(FP8X4), w3_planes[b][W3_ROW + 4 * a : P, :])
+            for e in range(ENTRY_TILES):
+                second[e] = keep.tile([P, KP], F32, name="second%d" % e, align_bytes=64)
+                nc.scalar.copy(second[e][:], sums2[e][:])
+            for e in range(ENTRY_TILES):
+                third[e] = keep.tile([P, PACK, P], F32, name=("page_grouped%d" if b else "third%d") % e, align_bytes=64)
+                nc.scalar.copy(dealt(third[e]), by_row(sums3[e]))
+
+        def first_product(b):
+            for e in range(ENTRY_TILES):
+                first[e] = bank(e)
+                least[e] = keep.tile([P, PACK, P], F32, name={(0, 3): "page_bf", (1, 0): "third2"}.get((b, e), "least%d" % e), align_bytes=64)
+            for a in range(PASSES):
+                for e in range(ENTRY_TILES):
+                    one_pass(first[e], e, a, w1_codes[a, b][:].bitcast(FP8X4), w1_scales[a, b][:])
+
+        def minimum(ts):
+            for e in range(ENTRY_TILES):
+                nc.vector.tensor_tensor(dealt(least[e])[:, :, ts], by_row(first[e])[:, :, ts], by_row(second[e])[:, :, ts], ALU.min)
+
+        def turn(s):
+            t = s % PACK
+            turned[s] = bank(ENTRY_TILES + t)
+            terms = [(term, e) for term in ((third, least) if s == 0 else (least, third)) for e in range(ENTRY_TILES)]
+            for n, (term, e) in enumerate(terms):
+                nc.tensor.matmul(
+                    turned[s][:, P * e : P * (e + 1)], lhsT=term[e][:, t, :], rhs=identity[:],
+                    start=(n == 0), stop=(n == len(terms) - 1), is_transpose=True,
+                )
+
+        def leave_bank(s):
+            if s == SLICES - 1:
+                h[s] = keep.tile([P, S], F32, name="page_grouped1", align_bytes=64)
+            elif s == PACK - 1:
+                h[s] = keep.tile([P, S], F32, name="third2", align_bytes=64)
+            else:
+                h[s] = keep.tile([P, S], F32, name="h%d" % (s % PACK), align_bytes=64)
+            nc.scalar.copy(h[s][:], turned[s][:])
+
+        page_bf, x_bf = {}, {}
+
+        def put_and_fetch(s):
+            put(s)
+            fetch(s)
+
+        def put(s):
+            nc.vector.tensor_tensor(page[s][:].indirect(list2[:]), h[s][:], wg[s % PACK], ALU.mult)
+
+        def fetch(s):
+            b, t = divmod(s, PACK)
+            if t == 0:
+                page_bf[b] = keep.tile([P, PACK, T2], BF16, name="page_bf", align_bytes=64)
+                x_bf[b] = keep.tile([P, PACK, NX], BF16, name="x_bf", align_bytes=64)
+            if s == PACK - 1:
+                shifted = keep.tile([P, NX], F32, name="second%d" % (ENTRY_TILES - 1), align_bytes=64)
+            elif s == PACK - 2:
+                shifted = keep.tile([P, NX], F32, name="third3", align_bytes=64)
+            else:
+                shifted = ring4.tile([P, NX], F32, name="shifted")
+            nc.vector.tensor_tensor(shifted[:], page[s][:].indirect(list3[:]), mats[s][:], ALU.add)
+            if s == SLICES - 1:
+                for c0 in range(0, T2, T2 // 2):
+                    nc.scalar.copy(page_bf[b][:, t, c0 : c0 + T2 // 2], page[s][:, c0 : c0 + T2 // 2])
+                nc.vector.tensor_scalar(x_bf[b][:, t, :], shifted[:], gv_sb[:, b, t : t + 1], None, ALU.mult)
+            else:
+                nc.scalar.copy(page_bf[b][:, t, :], page[s][:])
+                nc.scalar.activation(x_bf[b][:, t, :], shifted[:], ACT.Copy, scale=gv_sb[:, b, t : t + 1])
+
+        page_codes, page_scales, x_codes, x_scales = {}, {}, {}, {}
         x_grouped, page_grouped = {}, {}
 
-        def group_half(b):
-            last = b == HALVES - 1
-            x_grouped[b] = ring2.tile([P, NX * PACK], BF16, name="grouped", align_bytes=64)
-            interleave(nc.vector.tensor_copy if last else nc.scalar.copy, x_grouped[b][:], x_bf[b][:])
-            for c in range(T2 // CHUNK):
-                grouped = keep.tile([P, CHUNK * PACK], BF16, name="page_grouped%d" % c, align_bytes=64)
-                on_vector = last and c == T2 // CHUNK - 1
-                interleave(
-                    nc.vector.tensor_copy if on_vector else nc.scalar.copy, grouped[:], page_bf[b][:, :, CHUNK * c : CHUNK * (c + 1)]
-                )
-                page_grouped[b, c] = grouped
+        def group_x(b, copy):
+            x_grouped[b] = keep.tile([P, NX * PACK], BF16, name="grouped", align_bytes=64)
+            interleave(copy, x_grouped[b][:], x_bf[b][:])
 
-        def quantize_half(b):
+        def group_page(b, c, copy):
+            name = "grouped" if (b, c) == (HALVES - 1, CHUNKS - 1) else "page_grouped%d" % c
+            page_grouped[b, c] = keep.tile([P, CHUNK * PACK], BF16, name=name, align_bytes=64)
+            interleave(copy, page_grouped[b, c][:], page_bf[b][:, :, CHUNK * c : CHUNK * (c + 1)])
+
+        def quantize_x(b):
             x_codes[b] = keep.tile([P, NX], U32, name="x_codes%d" % b, align_bytes=64)
             x_scales[b] = keep.tile([P, NX], U8, name="x_scales%d" % b, align_bytes=64)
             nc.vector.quantize_mx(out=x_codes[b][:].bitcast(FP8X4), scales=x_scales[b][:], in_=x_grouped[b][:])
-            for c in range(T2 // CHUNK):
-                grouped = page_grouped[b, c]
-                page_codes[b, c] = keep.tile([P, CHUNK], U32, name="page_codes%d%d" % (b, c), align_bytes=64)
-                page_scales[b, c] = keep.tile([P, CHUNK], U8, name="page_scales%d%d" % (b, c), align_bytes=64)
-                nc.vector.quantize_mx(out=page_codes[b, c][:].bitcast(FP8X4), scales=page_scales[b, c][:], in_=grouped[:])
+
+        def quantize_page(b, c):
+            page_codes[b, c] = keep.tile([P, CHUNK], U32, name="page_codes%d%d" % (b, c), align_bytes=64)
+            page_scales[b, c] = keep.tile([P, CHUNK], U8, name="page_scales%d%d" % (b, c), align_bytes=64)
+            nc.vector.quantize_mx(out=page_codes[b, c][:].bitcast(FP8X4), scales=page_scales[b, c][:], in_=page_grouped[b, c][:])
 
         scores = {}
 
@@ -259,62 +294,89 @@ def tile_list_lottery_terminal_desk_kernel(
                     start=(b == 0), stop=(b == HALVES - 1),
                 )
 
-        grouped0 = round_w1(0, 0, P)
-        deal_w2(0)
-        quantize_w1(0, 0, grouped0)
-        quantize_w1(1, 0, round_w1(1, 0, 44))
-        deal_w3(0)
+        for a in range(PASSES):
+            for u in range(W1_PIECES):
+                grouped = ring2.tile([P, W1_COLS * PACK], BF16, name="w1_grouped", align_bytes=64)
+                round_w1(a, 0, u, nc.vector.tensor_copy, grouped)
+            quantize_w1(a, 0)
 
-        load_w1(0, 1)
-        load_w1(1, 1)
-        load_w3(1)
+        load_wg(wg_rest, slice(S, PACK * S))
+        load_page(1)
+        load_mat(1)
+        load_w1(0, 1, 0)
+        load_w1(0, 1, 1)
+        load_w2_planes(1)
+        load_page(2)
+        load_mat(2)
         load_w2(1)
-        load_wg(2)
-        load_slice(2)
-        load_wg(3)
+        load_w3(1)
+        load_w3_planes(1)
+        load_w1(1, 1, 0)
+        load_w1(1, 1, 1)
         for s in range(3, SLICES):
-            load_slice(s)
+            load_page(s)
+            load_mat(s)
         with nc.allow_non_contiguous_dma(reason="one value of slot for each output row"):
             nc.sync.dma_start(slot_sb[:], slot.rearrange("(n p) -> p n", p=P))
 
-        first_stage(0)
-        first_stage(1)
+        given_products(0)
+        first_product(0)
+        minimum(slice(0, 1))
+        turn(0)
+        leave_bank(0)
+        minimum(slice(1, PACK))
+        for s in range(1, PACK):
+            turn(s)
+        leave_bank(1)
+        leave_bank(2)
         put_and_fetch(0)
-        first_stage(2)
-        first_stage(3)
-        put_and_fetch(1)
-        grouped0 = round_w1(0, 1, P)
-        grouped1 = round_w1(1, 1, P)
-        deal_w2(1)
-        deal_w3(1)
-        quantize_w1(0, 1, grouped0)
-        quantize_w1(1, 1, grouped1)
-        put_and_fetch(2)
-        first_stage(4)
-        first_stage(5)
-        put_and_fetch(3)
-        first_stage(6)
-        products(7)
-        group_half(0)
+        for n, (a, u) in enumerate((a, u) for a in range(PASSES) for u in range(W1_PIECES)):
+            grouped = keep.tile([P, W1_COLS * PACK], BF16, name="third%d" % n, align_bytes=64)
+            round_w1(a, 1, u, nc.scalar.copy, grouped)
+        put(1)
+        quantize_w1(0, 1)
+        fetch(1)
+        put(2)
+        quantize_w1(1, 1)
+        leave_bank(3)
+        given_products(1)
+        fetch(2)
+        put(3)
+        first_product(1)
+        minimum(slice(0, PACK))
+        for s in range(PACK, SLICES):
+            turn(s)
+        leave_bank(4)
+        fetch(3)
+        leave_bank(5)
+        leave_bank(6)
+        group_x(0, nc.scalar.copy)
+        for c in range(CHUNKS):
+            group_page(0, c, nc.scalar.copy)
         put_and_fetch(4)
         put_and_fetch(5)
         put_and_fetch(6)
-        quantize_half(0)
-        combine(7)
+        quantize_x(0)
+        for c in range(CHUNKS):
+            quantize_page(0, c)
+        leave_bank(7)
         second_stage(0)
         put_and_fetch(7)
-        group_half(1)
-        quantize_half(1)
+        group_x(1, nc.vector.tensor_copy)
+        quantize_x(1)
+        for c in range(CHUNKS):
+            group_page(1, c, nc.vector.tensor_copy if c == CHUNKS - 1 else nc.scalar.copy)
+            quantize_page(1, c)
         second_stage(1)
 
         for n in range(T2 // P):
-            square = ring2.tile([P, NX], F32, name="square")
+            square = keep.tile([P, NX], F32, name="third%d" % (n % PACK), align_bytes=64)
             if n in SQUARES_ON_SCALAR:
                 nc.scalar.activation(square[:], scores[n][:], ACT.Square)
             else:
-                plain = ring2.tile([P, NX], F32, name="second")
+                plain = keep.tile([P, NX], F32, name="least%d" % (n % PACK), align_bytes=64)
                 nc.vector.tensor_copy(plain[:], scores[n][:])
                 nc.vector.tensor_tensor(square[:], scores[n][:], plain[:], ALU.mult)
-            result = ring4.tile([P, NX], F32, name="result")
+            result = keep.tile([P, NX], F32, name="result%d" % n if n >= PACK else "second%d" % n, align_bytes=64)
             nc.scalar.activation(result[:], square[:], ACT.Ln, bias=slot_sb[:, n : n + 1])
             nc.sync.dma_start(out[P * n : P * (n + 1), :], result[:])

@@ -59,10 +59,11 @@ def tile_list_lottery_terminal_desk_kernel(
         w2_codes = [keep.tile([P, PASSES, KP // 2], I32, name="w2_codes%d" % b, align_bytes=64) for b in range(HALVES)]
         w3_codes = [keep.tile([P, PASSES, KP], I32, name="w3_codes%d" % b, align_bytes=64) for b in range(HALVES)]
         wg_first = keep.tile([P, S], F32, name="wg_first")
-        wg_rest = keep.tile([P, (PACK - 1) * S], F32, name="wg_rest")
-        wg = [wg_first[:]] + [wg_rest[:, S * t : S * (t + 1)] for t in range(PACK - 1)]
+        wg_second = keep.tile([P, S], F32, name="wg_second")
+        wg_rest = keep.tile([P, 2 * S], F32, name="wg_rest")
+        wg = [wg_first[:], wg_second[:], wg_rest[:, :S], wg_rest[:, S:]]
         page = [keep.tile([P, T2], F32, name="page%d" % s) for s in range(SLICES)]
-        mats = [keep.tile([P, NX], F32, name="mat%d" % s) for s in range(SLICES)]
+        mats = [keep.tile([P, NX], F32, name="mat%d" % s, align_bytes=64) for s in range(SLICES)]
         gv_sb = keep.tile([P, HALVES, PACK], F32, name="gv_sb")
         slot_sb = keep.tile([P, T2 // P], F32, name="slot_sb")
         w1_raw = {}
@@ -157,7 +158,7 @@ def tile_list_lottery_terminal_desk_kernel(
             w1_grouped[a, b, u] = grouped
 
         def quantize_w1(a, b):
-            w1_codes[a, b] = keep.tile([P, KP], U32, name="h%d" % (a + 1) if b else "w1_codes%d" % a, align_bytes=64)
+            w1_codes[a, b] = keep.tile([P, KP], U32, name=("h1", "third1")[a] if b else "w1_codes%d" % a, align_bytes=64)
             w1_scales[a, b] = keep.tile([P, KP], U8, name="w1_scales%d%d" % (a, b), align_bytes=64)
             for u in range(W1_PIECES):
                 cols = slice(W1_COLS * u, W1_COLS * (u + 1))
@@ -183,25 +184,29 @@ def tile_list_lottery_terminal_desk_kernel(
 
         first, second, third, least, turned, h = {}, {}, {}, {}, {}, {}
 
-        def given_products(b):
-            sums2 = [bank(e) for e in range(ENTRY_TILES)]
-            sums3 = [bank(ENTRY_TILES + e) for e in range(ENTRY_TILES)]
+        def second_product(b):
+            sums = [bank(e) for e in range(ENTRY_TILES)]
             for a in range(PASSES):
                 for e in range(ENTRY_TILES):
-                    one_pass(sums2[e], e, a, w2_codes[b][:, a, :].bitcast(FP4X4), w2_planes[b][:, a, :])
-                for e in range(ENTRY_TILES):
-                    one_pass(sums3[e], e, a, w3_codes[b][:, a, :].bitcast(FP8X4), w3_planes[b][W3_ROW + 4 * a : P, :])
+                    one_pass(sums[e], e, a, w2_codes[b][:, a, :].bitcast(FP4X4), w2_planes[b][:, a, :])
             for e in range(ENTRY_TILES):
                 second[e] = keep.tile([P, KP], F32, name="second%d" % e, align_bytes=64)
-                nc.scalar.copy(second[e][:], sums2[e][:])
-            for e in range(ENTRY_TILES):
-                third[e] = keep.tile([P, PACK, P], F32, name=("page_grouped%d" if b else "third%d") % e, align_bytes=64)
-                nc.scalar.copy(dealt(third[e]), by_row(sums3[e]))
+                nc.scalar.copy(second[e][:], sums[e][:])
+
+        def third_product(b, entry_tiles):
+            sums = {e: bank(ENTRY_TILES + e % (3 if b else 4)) for e in entry_tiles}
+            for a in range(PASSES):
+                for e in entry_tiles:
+                    one_pass(sums[e], e, a, w3_codes[b][:, a, :].bitcast(FP8X4), w3_planes[b][W3_ROW + 4 * a : P, :])
+            for e in entry_tiles:
+                name = ("page_grouped0", "page_grouped1", "page_grouped2", "x_bf")[e] if b else "third%d" % e
+                third[e] = keep.tile([P, PACK, P], F32, name=name, align_bytes=64)
+                nc.scalar.copy(dealt(third[e]), by_row(sums[e]))
 
         def first_product(b):
             for e in range(ENTRY_TILES):
                 first[e] = bank(e)
-                least[e] = keep.tile([P, PACK, P], F32, name={(0, 3): "page_bf", (1, 0): "third2"}.get((b, e), "least%d" % e), align_bytes=64)
+                least[e] = keep.tile([P, PACK, P], F32, name={(0, 3): "page_bf", (1, 0): "third2", (1, 1): "second0", (1, 3): "page_grouped3"}.get((b, e), "least%d" % e), align_bytes=64)
             for a in range(PASSES):
                 for e in range(ENTRY_TILES):
                     one_pass(first[e], e, a, w1_codes[a, b][:].bitcast(FP8X4), w1_scales[a, b][:])
@@ -213,7 +218,7 @@ def tile_list_lottery_terminal_desk_kernel(
         def turn(s):
             t = s % PACK
             turned[s] = bank(ENTRY_TILES + t)
-            terms = [(term, e) for term in ((third, least) if s == 0 else (least, third)) for e in range(ENTRY_TILES)]
+            terms = [(term, e) for term in ((third, least) if t == 0 else (least, third)) for e in range(ENTRY_TILES)]
             for n, (term, e) in enumerate(terms):
                 nc.tensor.matmul(
                     turned[s][:, P * e : P * (e + 1)], lhsT=term[e][:, t, :], rhs=identity[:],
@@ -221,42 +226,36 @@ def tile_list_lottery_terminal_desk_kernel(
                 )
 
         def leave_bank(s):
-            if s == SLICES - 1:
-                h[s] = keep.tile([P, S], F32, name="page_grouped1", align_bytes=64)
-            elif s == PACK - 1:
-                h[s] = keep.tile([P, S], F32, name="third2", align_bytes=64)
-            else:
-                h[s] = keep.tile([P, S], F32, name="h%d" % (s % PACK), align_bytes=64)
+            name = {2: "third2", 3: "second1", 7: "page_grouped1"}.get(s, "h%d" % (s % PACK))
+            h[s] = keep.tile([P, S], F32, name=name, align_bytes=64)
             nc.scalar.copy(h[s][:], turned[s][:])
 
         page_bf, x_bf = {}, {}
 
-        def put_and_fetch(s):
-            put(s)
-            fetch(s)
+        shifted = {}
 
         def put(s):
             nc.vector.tensor_tensor(page[s][:].indirect(list2[:]), h[s][:], wg[s % PACK], ALU.mult)
 
         def fetch(s):
+            if s in (1, 2):
+                shifted[s] = keep.tile([P, NX], F32, name=("third3", "second3")[s - 1], align_bytes=64)
+            else:
+                shifted[s] = ring4.tile([P, NX], F32, name="shifted")
+            nc.vector.tensor_tensor(shifted[s][:], page[s][:].indirect(list3[:]), mats[s][:], ALU.add)
+
+        def round_slice(s):
             b, t = divmod(s, PACK)
             if t == 0:
                 page_bf[b] = keep.tile([P, PACK, T2], BF16, name="page_bf", align_bytes=64)
                 x_bf[b] = keep.tile([P, PACK, NX], BF16, name="x_bf", align_bytes=64)
-            if s == PACK - 1:
-                shifted = keep.tile([P, NX], F32, name="second%d" % (ENTRY_TILES - 1), align_bytes=64)
-            elif s == PACK - 2:
-                shifted = keep.tile([P, NX], F32, name="third3", align_bytes=64)
-            else:
-                shifted = ring4.tile([P, NX], F32, name="shifted")
-            nc.vector.tensor_tensor(shifted[:], page[s][:].indirect(list3[:]), mats[s][:], ALU.add)
             if s == SLICES - 1:
                 for c0 in range(0, T2, T2 // 2):
                     nc.scalar.copy(page_bf[b][:, t, c0 : c0 + T2 // 2], page[s][:, c0 : c0 + T2 // 2])
-                nc.vector.tensor_scalar(x_bf[b][:, t, :], shifted[:], gv_sb[:, b, t : t + 1], None, ALU.mult)
+                nc.vector.tensor_scalar(x_bf[b][:, t, :], shifted[s][:], gv_sb[:, b, t : t + 1], None, ALU.mult)
             else:
                 nc.scalar.copy(page_bf[b][:, t, :], page[s][:])
-                nc.scalar.activation(x_bf[b][:, t, :], shifted[:], ACT.Copy, scale=gv_sb[:, b, t : t + 1])
+                nc.scalar.activation(x_bf[b][:, t, :], shifted[s][:], ACT.Copy, scale=gv_sb[:, b, t : t + 1])
 
         page_codes, page_scales, x_codes, x_scales = {}, {}, {}, {}
         x_grouped, page_grouped = {}, {}
@@ -271,12 +270,13 @@ def tile_list_lottery_terminal_desk_kernel(
             interleave(copy, page_grouped[b, c][:], page_bf[b][:, :, CHUNK * c : CHUNK * (c + 1)])
 
         def quantize_x(b):
-            x_codes[b] = keep.tile([P, NX], U32, name="x_codes%d" % b, align_bytes=64)
+            x_codes[b] = keep.tile([P, NX], U32, name="x_codes" if b else "mat5", align_bytes=64)
             x_scales[b] = keep.tile([P, NX], U8, name="x_scales%d" % b, align_bytes=64)
             nc.vector.quantize_mx(out=x_codes[b][:].bitcast(FP8X4), scales=x_scales[b][:], in_=x_grouped[b][:])
 
         def quantize_page(b, c):
-            page_codes[b, c] = keep.tile([P, CHUNK], U32, name="page_codes%d%d" % (b, c), align_bytes=64)
+            name = {(0, 0): "mat4", (0, 3): "mat6"}.get((b, c), "page_codes%d%d" % (b, c))
+            page_codes[b, c] = keep.tile([P, CHUNK], U32, name=name, align_bytes=64)
             page_scales[b, c] = keep.tile([P, CHUNK], U8, name="page_scales%d%d" % (b, c), align_bytes=64)
             nc.vector.quantize_mx(out=page_codes[b, c][:].bitcast(FP8X4), scales=page_scales[b, c][:], in_=page_grouped[b, c][:])
 
@@ -300,26 +300,27 @@ def tile_list_lottery_terminal_desk_kernel(
                 round_w1(a, 0, u, nc.vector.tensor_copy, grouped)
             quantize_w1(a, 0)
 
-        load_wg(wg_rest, slice(S, PACK * S))
+        for a in range(PASSES):
+            for u in range(W1_PIECES):
+                load_w1(a, 1, u)
+        load_wg(wg_second, slice(S, 2 * S))
         load_page(1)
         load_mat(1)
-        load_w1(0, 1, 0)
-        load_w1(0, 1, 1)
+        load_w2(1)
         load_w2_planes(1)
+        load_wg(wg_rest, slice(2 * S, PACK * S))
         load_page(2)
         load_mat(2)
-        load_w2(1)
         load_w3(1)
         load_w3_planes(1)
-        load_w1(1, 1, 0)
-        load_w1(1, 1, 1)
         for s in range(3, SLICES):
             load_page(s)
             load_mat(s)
         with nc.allow_non_contiguous_dma(reason="one value of slot for each output row"):
             nc.sync.dma_start(slot_sb[:], slot.rearrange("(n p) -> p n", p=P))
 
-        given_products(0)
+        second_product(0)
+        third_product(0, range(ENTRY_TILES))
         first_product(0)
         minimum(slice(0, 1))
         turn(0)
@@ -328,40 +329,47 @@ def tile_list_lottery_terminal_desk_kernel(
         for s in range(1, PACK):
             turn(s)
         leave_bank(1)
-        leave_bank(2)
-        put_and_fetch(0)
         for n, (a, u) in enumerate((a, u) for a in range(PASSES) for u in range(W1_PIECES)):
-            grouped = keep.tile([P, W1_COLS * PACK], BF16, name="third%d" % n, align_bytes=64)
+            grouped = keep.tile([P, W1_COLS * PACK], BF16, name="third%d" % n if n else "page_bf", align_bytes=64)
             round_w1(a, 1, u, nc.scalar.copy, grouped)
+        put(0)
+        fetch(0)
         put(1)
         quantize_w1(0, 1)
+        quantize_w1(1, 1)
+        leave_bank(2)
+        second_product(1)
         fetch(1)
         put(2)
-        quantize_w1(1, 1)
-        leave_bank(3)
-        given_products(1)
-        fetch(2)
-        put(3)
         first_product(1)
+        third_product(1, range(3))
+        third_product(1, range(3, 4))
         minimum(slice(0, PACK))
+        leave_bank(3)
+        fetch(2)
         for s in range(PACK, SLICES):
             turn(s)
-        leave_bank(4)
+        for s in range(PACK, SLICES - 1):
+            leave_bank(s)
+        put(3)
         fetch(3)
-        leave_bank(5)
-        leave_bank(6)
+        for s in range(PACK):
+            round_slice(s)
         group_x(0, nc.scalar.copy)
         for c in range(CHUNKS):
             group_page(0, c, nc.scalar.copy)
-        put_and_fetch(4)
-        put_and_fetch(5)
-        put_and_fetch(6)
+        for s in range(PACK, SLICES - 1):
+            put(s)
+            fetch(s)
+            round_slice(s)
         quantize_x(0)
         for c in range(CHUNKS):
             quantize_page(0, c)
         leave_bank(7)
         second_stage(0)
-        put_and_fetch(7)
+        put(7)
+        fetch(7)
+        round_slice(7)
         group_x(1, nc.vector.tensor_copy)
         quantize_x(1)
         for c in range(CHUNKS):

from contextlib import ExitStack

import concourse.mybir as mybir
from concourse.masks import make_identity

K, H, T, S, T2, NX = 1024, 1024, 2048, 512, 1024, 512
FLOPS = 2 * (3 * K * H * S + H * T2 * NX)

F32 = mybir.dt.float32
BF16 = mybir.dt.bfloat16
I32 = mybir.dt.int32
U32 = mybir.dt.uint32
U16 = mybir.dt.uint16
U8 = mybir.dt.uint8
FP8X4 = mybir.dt.float8_e4m3fn_x4
FP4X4 = mybir.dt.float4_e2m1fn_x4
ALU = mybir.AluOpType
ACT = mybir.ActivationFunctionType

P = 128
PACK = 4
KP = P * PACK
PASSES = K // KP
HALVES = H // KP
SLICES = HALVES * PACK
ENTRY_TILES = S // P
CHUNK = 256
CHUNKS = T2 // CHUNK
W1_COLS = 256
W1_PIECES = KP // W1_COLS
W3_ROW = 8
SQUARES_ON_SCALAR = (0, 1, 3, 5)


def tile_list_lottery_terminal_desk_kernel(
    tc, tab_words, tab_scales, offs, offs2, offs3, w1, w2_words, w2_scales, w3_words, w3_scales, wgs, page0, mat, gv, slot, out
):
    nc = tc.nc
    with ExitStack() as ctx:
        keep = ctx.enter_context(tc.tile_pool(name="keep", bufs=1))
        ring2 = ctx.enter_context(tc.tile_pool(name="ring2", bufs=2))
        ring4 = ctx.enter_context(tc.tile_pool(name="ring4", bufs=4))
        psum = ctx.enter_context(tc.psum_pool(name="psum", bufs=1))

        list1 = keep.tile([P, S // 16], U16, name="list1")
        list2 = keep.tile([P, S // 16], U16, name="list2")
        list3 = keep.tile([P, NX // 16], U16, name="list3")
        tab_w = [keep.tile([P, T], I32, name="tab_w%d" % a, align_bytes=64) for a in range(PASSES)]
        tab_s = keep.tile([P, PASSES * T], U8, name="tab_s", align_bytes=64)
        w2_planes = [keep.tile([P, PASSES, KP], U8, name="w2_planes%d" % b, align_bytes=64) for b in range(HALVES)]
        w3_planes = [keep.tile([P, KP], U8, name="w3_planes%d" % b, align_bytes=64) for b in range(HALVES)]
        nc.gpsimd.memset(tab_s[:].bitcast(I32), 0)
        for planes in (w2_planes[0], w3_planes[0], w2_planes[1], w3_planes[1]):
            nc.vector.memset(planes[:].bitcast(I32), 0)
        warm = keep.tile([P, 2], F32, name="warm")
        nc.vector.memset(warm[:], 1.0)
        nc.scalar.activation(warm[:, 1:2], warm[:, 0:1], ACT.Ln)

        w2_codes = [keep.tile([P, PASSES, KP // 2], I32, name="w2_codes%d" % b, align_bytes=64) for b in range(HALVES)]
        w3_codes = [keep.tile([P, PASSES, KP], I32, name="w3_codes%d" % b, align_bytes=64) for b in range(HALVES)]
        wg_first = keep.tile([P, S], F32, name="wg_first")
        wg_second = keep.tile([P, S], F32, name="wg_second")
        wg_rest = keep.tile([P, 2 * S], F32, name="wg_rest")
        wg = [wg_first[:], wg_second[:], wg_rest[:, :S], wg_rest[:, S:]]
        page = [keep.tile([P, T2], F32, name="page%d" % s) for s in range(SLICES)]
        mats = [keep.tile([P, NX], F32, name="mat%d" % s, align_bytes=64) for s in range(SLICES)]
        gv_sb = keep.tile([P, HALVES, PACK], F32, name="gv_sb")
        slot_sb = keep.tile([P, T2 // P], F32, name="slot_sb")
        w1_raw = {}

        def load_tab(a):
            nc.sync.dma_start(tab_w[a][:], tab_words[a].rearrange("p n i -> p (n i)").bitcast(I32))

        def load_tab_scales():
            for r in range(4):
                nc.sync.dma_start(
                    tab_s[r:P:32, :].bitcast(I32).rearrange("q (a n) -> q a n", a=PASSES),
                    tab_scales.rearrange("a (q r) n -> r q a n", r=4)[r].bitcast(I32),
                )

        def load_w2_planes(b):
            for r in range(4):
                nc.sync.dma_start(
                    w2_planes[b][r:P:32, :, :].bitcast(I32),
                    w2_scales.rearrange("a (q r) n -> r q a n", r=4)[r][:, :, KP * b : KP * (b + 1)].bitcast(I32),
                )

        def load_w3_planes(b):
            for q in range(4):
                nc.sync.dma_start(
                    w3_planes[b][32 * q + W3_ROW : 32 * q + W3_ROW + 8, :].bitcast(I32),
                    w3_scales[:, 4 * q : 4 * q + 4, KP * b : KP * (b + 1)].bitcast(I32),
                )

        def load_wg(tile, cols):
            rows = wgs.rearrange("(p t) j -> p (t j)", t=PACK)[:, cols]
            for q in range(4):
                nc.sync.dma_start(tile[32 * q : 32 * (q + 1), :], rows)

        def load_w1(a, b, u):
            w1_raw[a, b, u] = keep.tile([P, PACK, W1_COLS], F32, name="w1_raw%d%d%d" % (a, b, u))
            c0 = KP * b + W1_COLS * u
            rows = w1[KP * a : KP * (a + 1), c0 : c0 + W1_COLS]
            nc.sync.dma_start(w1_raw[a, b, u][:], rows.rearrange("(p j) c -> p j c", j=PACK))

        def load_w3(b):
            nc.sync.dma_start(
                w3_codes[b][:], w3_words.rearrange("a p c i -> p a (c i)")[:, :, 4 * KP * b : 4 * KP * (b + 1)].bitcast(I32)
            )

        def load_w2(b):
            nc.sync.dma_start(
                w2_codes[b][:], w2_words.rearrange("a p c -> p a c")[:, :, 2 * KP * b : 2 * KP * (b + 1)].bitcast(I32)
            )

        def load_page(s):
            b, t = divmod(s, PACK)
            nc.sync.dma_start(page[s][:], page0.rearrange("(b p t) m -> b t p m", b=HALVES, t=PACK)[b, t])

        def load_mat(s):
            b, t = divmod(s, PACK)
            nc.sync.dma_start(mats[s][:], mat.rearrange("(b p t) j -> b t p j", b=HALVES, t=PACK)[b, t])

        nc.sync.dma_start(list1[:], offs)
        load_tab(0)
        load_tab_scales()
        load_tab(1)
        load_w2(0)
        load_w2_planes(0)
        load_w3(0)
        load_w1(0, 0, 0)
        load_w3_planes(0)
        load_w1(0, 0, 1)
        load_w1(1, 0, 0)
        load_w1(1, 0, 1)
        identity = keep.tile([P, P], F32, name="identity")
        make_identity(nc, identity[:])
        nc.sync.dma_start(list2[:], offs2)
        nc.sync.dma_start(gv_sb[:], gv.rearrange("(b p t) -> p b t", b=HALVES, t=PACK))
        load_page(0)
        load_wg(wg_first, slice(0, S))
        nc.sync.dma_start(list3[:], offs3)
        load_mat(0)

        v_codes = [keep.tile([P, S], U32, name="v_codes%d" % a, align_bytes=64) for a in range(PASSES)]
        v_scales = [keep.tile([P, S], U8, name="v_scales%d" % a, align_bytes=64) for a in range(PASSES)]
        for a in range(PASSES):
            nc.vector.tensor_copy(v_codes[a][:], tab_w[a][:].bitcast(U32).indirect(list1[:]))
            nc.vector.tensor_copy(v_scales[a][:], tab_s[:, T * a : T * (a + 1)].indirect(list1[:]))

        def interleave(copy, dst, src):
            copy(dst.rearrange("p (c i t) -> p c t i", t=PACK, i=4), src.rearrange("p t (c i) -> p c t i", i=4))

        w1_codes, w1_scales, w1_grouped = {}, {}, {}

        def round_w1(a, b, u, copy, grouped):
            interleave(copy, grouped[:], w1_raw[a, b, u][:])
            w1_grouped[a, b, u] = grouped

        def quantize_w1(a, b):
            w1_codes[a, b] = keep.tile([P, KP], U32, name=("h1", "third1")[a] if b else "w1_codes%d" % a, align_bytes=64)
            w1_scales[a, b] = keep.tile([P, KP], U8, name="w1_scales%d%d" % (a, b), align_bytes=64)
            for u in range(W1_PIECES):
                cols = slice(W1_COLS * u, W1_COLS * (u + 1))
                nc.vector.quantize_mx(
                    out=w1_codes[a, b][:, cols].bitcast(FP8X4), scales=w1_scales[a, b][:, cols], in_=w1_grouped[a, b, u][:]
                )

        def bank(n):
            return psum.tile([P, 512], F32, name="bank%d" % n)

        def by_row(tile):
            return tile[:].rearrange("p (m t) -> p m t", t=PACK)

        def dealt(tile):
            return tile[:].rearrange("p t m -> p m t")

        def one_pass(acc, e, a, codes, scales):
            entries = slice(P * e, P * (e + 1))
            nc.tensor.matmul_mx(
                out=acc[:], lhsT=v_codes[a][:, entries].bitcast(FP8X4), lhsT_scale=v_scales[a][:, entries],
                rhs=codes, rhs_scale=scales, start=(a == 0), stop=(a == PASSES - 1),
            )

        first, second, third, least, turned, h = {}, {}, {}, {}, {}, {}

        def second_product(b):
            sums = [bank(e) for e in range(ENTRY_TILES)]
            for a in range(PASSES):
                for e in range(ENTRY_TILES):
                    one_pass(sums[e], e, a, w2_codes[b][:, a, :].bitcast(FP4X4), w2_planes[b][:, a, :])
            for e in range(ENTRY_TILES):
                second[e] = keep.tile([P, KP], F32, name="second%d" % e, align_bytes=64)
                nc.scalar.copy(second[e][:], sums[e][:])

        def third_product(b, entry_tiles):
            sums = {e: bank(ENTRY_TILES + e % (3 if b else 4)) for e in entry_tiles}
            for a in range(PASSES):
                for e in entry_tiles:
                    one_pass(sums[e], e, a, w3_codes[b][:, a, :].bitcast(FP8X4), w3_planes[b][W3_ROW + 4 * a : P, :])
            for e in entry_tiles:
                name = ("page_grouped0", "page_grouped1", "page_grouped2", "x_bf")[e] if b else "third%d" % e
                third[e] = keep.tile([P, PACK, P], F32, name=name, align_bytes=64)
                nc.scalar.copy(dealt(third[e]), by_row(sums[e]))

        def first_product(b):
            for e in range(ENTRY_TILES):
                first[e] = bank(e)
                least[e] = keep.tile([P, PACK, P], F32, name={(0, 3): "page_bf", (1, 0): "third2", (1, 1): "second0", (1, 3): "page_grouped3"}.get((b, e), "least%d" % e), align_bytes=64)
            for a in range(PASSES):
                for e in range(ENTRY_TILES):
                    one_pass(first[e], e, a, w1_codes[a, b][:].bitcast(FP8X4), w1_scales[a, b][:])

        def minimum(ts):
            for e in range(ENTRY_TILES):
                nc.vector.tensor_tensor(dealt(least[e])[:, :, ts], by_row(first[e])[:, :, ts], by_row(second[e])[:, :, ts], ALU.min)

        def turn(s):
            t = s % PACK
            turned[s] = bank(ENTRY_TILES + t)
            terms = [(term, e) for term in ((third, least) if t == 0 else (least, third)) for e in range(ENTRY_TILES)]
            for n, (term, e) in enumerate(terms):
                nc.tensor.matmul(
                    turned[s][:, P * e : P * (e + 1)], lhsT=term[e][:, t, :], rhs=identity[:],
                    start=(n == 0), stop=(n == len(terms) - 1), is_transpose=True,
                )

        def leave_bank(s):
            name = {2: "third2", 3: "second1", 7: "page_grouped1"}.get(s, "h%d" % (s % PACK))
            h[s] = keep.tile([P, S], F32, name=name, align_bytes=64)
            nc.scalar.copy(h[s][:], turned[s][:])

        page_bf, x_bf = {}, {}

        shifted = {}

        def put(s):
            nc.vector.tensor_tensor(page[s][:].indirect(list2[:]), h[s][:], wg[s % PACK], ALU.mult)

        def fetch(s):
            if s in (1, 2):
                shifted[s] = keep.tile([P, NX], F32, name=("third3", "second3")[s - 1], align_bytes=64)
            else:
                shifted[s] = ring4.tile([P, NX], F32, name="shifted")
            nc.vector.tensor_tensor(shifted[s][:], page[s][:].indirect(list3[:]), mats[s][:], ALU.add)

        def round_slice(s):
            b, t = divmod(s, PACK)
            if t == 0:
                page_bf[b] = keep.tile([P, PACK, T2], BF16, name="page_bf", align_bytes=64)
                x_bf[b] = keep.tile([P, PACK, NX], BF16, name="x_bf", align_bytes=64)
            if s == SLICES - 1:
                for c0 in range(0, T2, T2 // 2):
                    nc.scalar.copy(page_bf[b][:, t, c0 : c0 + T2 // 2], page[s][:, c0 : c0 + T2 // 2])
                nc.vector.tensor_scalar(x_bf[b][:, t, :], shifted[s][:], gv_sb[:, b, t : t + 1], None, ALU.mult)
            else:
                nc.scalar.copy(page_bf[b][:, t, :], page[s][:])
                nc.scalar.activation(x_bf[b][:, t, :], shifted[s][:], ACT.Copy, scale=gv_sb[:, b, t : t + 1])

        page_codes, page_scales, x_codes, x_scales = {}, {}, {}, {}
        x_grouped, page_grouped = {}, {}

        def group_x(b, copy):
            x_grouped[b] = keep.tile([P, NX * PACK], BF16, name="grouped", align_bytes=64)
            interleave(copy, x_grouped[b][:], x_bf[b][:])

        def group_page(b, c, copy):
            name = "grouped" if (b, c) == (HALVES - 1, CHUNKS - 1) else "page_grouped%d" % c
            page_grouped[b, c] = keep.tile([P, CHUNK * PACK], BF16, name=name, align_bytes=64)
            interleave(copy, page_grouped[b, c][:], page_bf[b][:, :, CHUNK * c : CHUNK * (c + 1)])

        def quantize_x(b):
            x_codes[b] = keep.tile([P, NX], U32, name="x_codes" if b else "mat5", align_bytes=64)
            x_scales[b] = keep.tile([P, NX], U8, name="x_scales%d" % b, align_bytes=64)
            nc.vector.quantize_mx(out=x_codes[b][:].bitcast(FP8X4), scales=x_scales[b][:], in_=x_grouped[b][:])

        def quantize_page(b, c):
            name = {(0, 0): "mat4", (0, 3): "mat6"}.get((b, c), "page_codes%d%d" % (b, c))
            page_codes[b, c] = keep.tile([P, CHUNK], U32, name=name, align_bytes=64)
            page_scales[b, c] = keep.tile([P, CHUNK], U8, name="page_scales%d%d" % (b, c), align_bytes=64)
            nc.vector.quantize_mx(out=page_codes[b, c][:].bitcast(FP8X4), scales=page_scales[b, c][:], in_=page_grouped[b, c][:])

        scores = {}

        def second_stage(b):
            for n in range(T2 // P):
                c, off = divmod(P * n, CHUNK)
                if b == 0:
                    scores[n] = bank(n)
                nc.tensor.matmul_mx(
                    out=scores[n][:],
                    lhsT=page_codes[b, c][:, off : off + P].bitcast(FP8X4), lhsT_scale=page_scales[b, c][:, off : off + P],
                    rhs=x_codes[b][:].bitcast(FP8X4), rhs_scale=x_scales[b][:],
                    start=(b == 0), stop=(b == HALVES - 1),
                )

        for a in range(PASSES):
            for u in range(W1_PIECES):
                grouped = ring2.tile([P, W1_COLS * PACK], BF16, name="w1_grouped", align_bytes=64)
                round_w1(a, 0, u, nc.vector.tensor_copy, grouped)
            quantize_w1(a, 0)

        for a in range(PASSES):
            for u in range(W1_PIECES):
                load_w1(a, 1, u)
        load_wg(wg_second, slice(S, 2 * S))
        load_page(1)
        load_mat(1)
        load_w2(1)
        load_w2_planes(1)
        load_wg(wg_rest, slice(2 * S, PACK * S))
        load_page(2)
        load_mat(2)
        load_w3(1)
        load_w3_planes(1)
        for s in range(3, SLICES):
            load_page(s)
            load_mat(s)
        with nc.allow_non_contiguous_dma(reason="one value of slot for each output row"):
            nc.sync.dma_start(slot_sb[:], slot.rearrange("(n p) -> p n", p=P))

        second_product(0)
        third_product(0, range(ENTRY_TILES))
        first_product(0)
        minimum(slice(0, 1))
        turn(0)
        leave_bank(0)
        minimum(slice(1, PACK))
        for s in range(1, PACK):
            turn(s)
        leave_bank(1)
        for n, (a, u) in enumerate((a, u) for a in range(PASSES) for u in range(W1_PIECES)):
            grouped = keep.tile([P, W1_COLS * PACK], BF16, name="third%d" % n if n else "page_bf", align_bytes=64)
            round_w1(a, 1, u, nc.scalar.copy, grouped)
        put(0)
        fetch(0)
        put(1)
        quantize_w1(0, 1)
        quantize_w1(1, 1)
        leave_bank(2)
        second_product(1)
        fetch(1)
        put(2)
        first_product(1)
        third_product(1, range(3))
        third_product(1, range(3, 4))
        minimum(slice(0, PACK))
        leave_bank(3)
        fetch(2)
        for s in range(PACK, SLICES):
            turn(s)
        for s in range(PACK, SLICES - 1):
            leave_bank(s)
        put(3)
        fetch(3)
        for s in range(PACK):
            round_slice(s)
        group_x(0, nc.scalar.copy)
        for c in range(CHUNKS):
            group_page(0, c, nc.scalar.copy)
        for s in range(PACK, SLICES - 1):
            put(s)
            fetch(s)
            round_slice(s)
        quantize_x(0)
        for c in range(CHUNKS):
            quantize_page(0, c)
        leave_bank(7)
        second_stage(0)
        put(7)
        fetch(7)
        round_slice(7)
        group_x(1, nc.vector.tensor_copy)
        quantize_x(1)
        for c in range(CHUNKS):
            group_page(1, c, nc.vector.tensor_copy if c == CHUNKS - 1 else nc.scalar.copy)
            quantize_page(1, c)
        second_stage(1)

        for n in range(T2 // P):
            square = keep.tile([P, NX], F32, name="third%d" % (n % PACK), align_bytes=64)
            if n in SQUARES_ON_SCALAR:
                nc.scalar.activation(square[:], scores[n][:], ACT.Square)
            else:
                plain = keep.tile([P, NX], F32, name="least%d" % (n % PACK), align_bytes=64)
                nc.vector.tensor_copy(plain[:], scores[n][:])
                nc.vector.tensor_tensor(square[:], scores[n][:], plain[:], ALU.mult)
            result = keep.tile([P, NX], F32, name="result%d" % n if n >= PACK else "second%d" % n, align_bytes=64)
            nc.scalar.activation(result[:], square[:], ACT.Ln, bias=slot_sb[:, n : n + 1])
            nc.sync.dma_start(out[P * n : P * (n + 1), :], result[:])
